import numpy as np
import ml_dtypes


def mxq(x, axis, fmt="e4m3"):
    dtype, down = {"e4m3": (ml_dtypes.float8_e4m3fn, 7), "e5m2": (ml_dtypes.float8_e5m2, 14)}[fmt]
    v = np.moveaxis(np.asarray(x, np.float32).astype(ml_dtypes.bfloat16).astype(np.float64), axis, -1)
    blocks = v.reshape(v.shape[:-1] + (-1, 32))
    amax = np.abs(blocks).max(-1, keepdims=True)
    byte = np.maximum(np.where(amax > 0, np.frexp(amax)[1] - 1 + 127, 0) - down, 1)
    scale = np.exp2(byte - 127.0)
    codes = (blocks / scale).astype(np.float32).astype(dtype).astype(np.float64)
    return np.moveaxis((codes * scale).reshape(v.shape), -1, axis)


WIDE = False


def mx_kscale(k):
    if not WIDE:
        return np.ones(k)
    levels = np.array([10, -10, 5, -5, 0])
    if k % 512:
        return np.exp2(np.random.permutation(np.resize(levels, k // 32))).repeat(32)
    a = np.empty((k // 512, 16))
    for p in range(k // 512):
        a[p, :8] = np.random.permutation(np.resize(levels, 8))
        for g in range(8):
            far = levels[np.abs(levels - a[p, g]) >= 10]
            a[p, g + 8] = far[np.random.randint(len(far))]
    return np.exp2(a.ravel()).repeat(32)


def f64(x):
    return np.asarray(x).astype(np.float64)


def striped(idx):
    return np.tile(idx.reshape(-1, 16).T, (8, 1)).astype(np.uint16)


def unstriped(offs):
    return offs[:16].T.reshape(-1).astype(np.int64)


def pack_weight(w):
    k, n = w.shape
    w = f64(np.asarray(w, np.float32).astype(ml_dtypes.bfloat16)).reshape(k // 32, 32, n)
    amax = np.abs(w).max(1)
    byte = np.clip(np.where(amax > 0, np.frexp(amax)[1] - 1 + 127 - 7, 1), 1, 254)
    scaled = (w * np.exp2(127.0 - byte)[:, None, :]).reshape(k, n).astype(np.float32)
    words = np.ascontiguousarray(scaled.reshape(k // 512, 128, 4, n).transpose(0, 1, 3, 2)).astype(ml_dtypes.float8_e4m3fn).view(np.uint8)
    return words, np.ascontiguousarray(byte.astype(np.uint8).reshape(k // 512, 16, n))


def unpack_weight(words, scales):
    g, p, n, _ = words.shape
    vals = np.ascontiguousarray(words).view(ml_dtypes.float8_e4m3fn).astype(np.float64) * np.repeat(np.exp2(scales.astype(np.float64) - 127.0), 8, axis=1)[..., None]
    return vals.transpose(0, 1, 3, 2).reshape(g * 512, n)


K, T, S, N, H = 512, 2048, 512, 128, 512


def setup_inputs():
    n = np.random.standard_normal
    s = mx_kscale(K)[:, None]
    u = mx_kscale(H)
    packed_xT = pack_weight(n((K, T)) * s)
    return {
        "x_words": packed_xT[0],
        "x_scales": packed_xT[1],
        "hT": (n((K, H)) / np.sqrt(K) / s).astype(np.float32),
        "unit": (np.random.uniform(0.6, 1.4, (H, 1)) * u[:, None]).astype(np.float32),
        "w1": (n((H, N)) / np.sqrt(H) / u[:, None]).astype(np.float32),
        "offs": striped(np.random.permutation(T)[:S]),
        "cit": striped(np.random.permutation(S)),
    }


def reference(x_words, x_scales, hT, unit, w1, offs, cit):
    hTq = mxq(f64(hT), 0, "e4m3")
    xq = unpack_weight(x_words, x_scales)[:, unstriped(offs)]
    y = hTq.T @ xq
    ker = np.exp(1.2 * np.tanh(y))
    pop = ker.mean(axis=1, keepdims=True)
    cal = ker / (pop + 0.3)
    zc = cal[:, unstriped(cit)]
    prop = cal + 0.6 * zc
    hid = f64(unit) * (np.log(prop + 0.3) * y)
    return mxq(f64(w1), 0, "e4m3").T @ mxq(hid, 0, "e4m3")

@@ -1,0 +1,191 @@
+from contextlib import ExitStack
+
+import concourse.mybir as mybir
+
+K, T, S, N, H = 512, 2048, 512, 128, 512
+FLOPS = 2 * K * H * S + 2 * H * N * S
+
+F32 = mybir.dt.float32
+BF16 = mybir.dt.bfloat16
+I32 = mybir.dt.int32
+U32 = mybir.dt.uint32
+U16 = mybir.dt.uint16
+U8 = mybir.dt.uint8
+FP8X4 = mybir.dt.float8_e4m3fn_x4
+ACT = mybir.ActivationFunctionType
+MULT = mybir.AluOpType.mult
+ADD = mybir.AluOpType.add
+
+P = 128
+PACK = 4
+HALF = S // 2
+SPARE = 192
+
+
+def tile_picked_yanchr_log_p_kernel(tc, x_words, x_scales, hT, unit, w1, offs, cit, out):
+    nc = tc.nc
+    with ExitStack() as ctx:
+        keep = ctx.enter_context(tc.tile_pool(name="keep", bufs=1))
+        psum = ctx.enter_context(tc.psum_pool(name="psum", bufs=1))
+
+        halves = [slice(0, HALF), slice(HALF, S)]
+
+        offs_sb = keep.tile([P, S // 16], U16, name="offs_sb")
+        cit_sb = keep.tile([P, S // 16], U16, name="cit_sb")
+        x_bytes = keep.tile([P, T], U8, name="x_bytes", align_bytes=64)
+        x_table = keep.tile([P, T], I32, name="x_table", align_bytes=64)
+        h_raw = keep.tile([P, PACK, H], F32, name="h_raw", align_bytes=64)
+        w_raw = keep.tile([P, PACK, N], F32, name="w_raw", align_bytes=64)
+        unit_sb = keep.tile([P, PACK], F32, name="unit_sb")
+
+        nc.gpsimd.memset(x_bytes[:].bitcast(I32), 0)
+        nc.sync.dma_start(offs_sb[:], offs)
+        for q in range(4):
+            nc.scalar.dma_start(x_bytes[32 * q : 32 * q + 4, :].bitcast(I32), x_scales[0, 4 * q : 4 * q + 4, :].bitcast(I32))
+        nc.sync.dma_start(h_raw[:], hT.rearrange("(p j) i -> p j i", j=PACK))
+        nc.sync.dma_start(x_table[:], x_words[0].rearrange("p n t -> p (n t)").bitcast(I32))
+        nc.sync.dma_start(cit_sb[:], cit)
+        nc.sync.dma_start(w_raw[:], w1.rearrange("(p j) m -> p j m", j=PACK))
+        nc.sync.dma_start(unit_sb[:], unit.rearrange("(p t) o -> p (t o)", t=PACK))
+
+        ker = keep.tile([P, PACK * S + SPARE], F32, name="ker", align_bytes=64)
+        nc.gpsimd.memset(ker[:, PACK * S :], 0.0)
+
+        h_view = h_raw[:].rearrange("p j (m t) -> p m t j", t=PACK)
+        h_codes, h_scales = [], []
+        h_bf = []
+        for pair in range(2):
+            h_bf.append(keep.tile([P, 2, P, PACK], BF16, name="h_bf%d" % pair, align_bytes=64))
+            h_codes.append(keep.tile([P, 2 * P], U32, name="h_codes%d" % pair, align_bytes=64))
+            h_scales.append(keep.tile([P, 2 * P], U8, name="h_scales%d" % pair, align_bytes=64))
+        nc.vector.tensor_copy(h_bf[0][:].rearrange("p t m j -> p m t j"), h_view[:, :, 0:2, :])
+        nc.scalar.activation(h_bf[1][:].rearrange("p t m j -> p m t j"), h_view[:, :, 2:4, :], ACT.Copy)
+        nc.vector.quantize_mx(h_codes[0][:].bitcast(FP8X4), h_scales[0][:], h_bf[0][:].rearrange("p t m j -> p (t m j)"))
+
+        picked_bytes = keep.tile([P, S], U8, name="picked_bytes", align_bytes=64)
+        nc.vector.tensor_copy(picked_bytes[:], x_bytes[:].indirect(offs_sb[:]))
+        picked_words = []
+        for h in range(2):
+            words = keep.tile([P, HALF], U32, name="picked_words%d" % h, align_bytes=64)
+            nc.vector.tensor_copy(words[:], x_table[:].bitcast(U32).indirect(offs_sb[:, 16 * h : 16 * h + 16]))
+            picked_words.append(words)
+        nc.vector.quantize_mx(h_codes[1][:].bitcast(FP8X4), h_scales[1][:], h_bf[1][:].rearrange("p t m j -> p (t m j)"))
+
+        y = {}
+        for t in range(2):
+            for h in range(2):
+                y[t, h] = psum.tile([P, HALF], F32, name="y%d%d" % (t, h))[:]
+        for t in range(2, 4):
+            bank = psum.tile([P, S], F32, name="y%d" % t)
+            y[t] = bank
+            for h in range(2):
+                y[t, h] = bank[:, halves[h]]
+
+        def product(t, h):
+            cols = slice((t % 2) * P, (t % 2 + 1) * P)
+            nc.tensor.matmul_mx(
+                y[t, h],
+                lhsT=h_codes[t // 2][:, cols].bitcast(FP8X4),
+                lhsT_scale=h_scales[t // 2][:, cols],
+                rhs=picked_words[h][:].bitcast(FP8X4),
+                rhs_scale=picked_bytes[:, halves[h]],
+                start=True,
+                stop=True,
+            )
+
+        for t, h in ((0, 0), (1, 0), (0, 1), (1, 1), (2, 0), (2, 1), (3, 0), (3, 1)):
+            product(t, h)
+
+        w_bf = keep.tile([P, N, PACK], BF16, name="w_bf", align_bytes=64)
+        w_codes = keep.tile([P, N], U32, name="w_codes", align_bytes=64)
+        w_scales = keep.tile([P, N], U8, name="w_scales", align_bytes=64)
+        nc.vector.tensor_copy(
+            w_bf[:].rearrange("p (c i) j -> p c j i", i=4), w_raw[:].rearrange("p j (c i) -> p c j i", i=4)
+        )
+        nc.vector.quantize_mx(w_codes[:].bitcast(FP8X4), w_scales[:], w_bf[:].rearrange("p m j -> p (m j)"))
+
+        logs = keep.tile([P, PACK, S], F32, name="logs", align_bytes=64)
+        th = [keep.tile([P, S], F32, name="th%d" % t, align_bytes=64) for t in range(3)]
+        last_th = logs[:].rearrange("p t (h c) -> p (t h) c", h=2)[:, :, 0:64]
+        sums = keep.tile([P, PACK], F32, name="sums")
+        shifted = keep.tile([P, PACK], F32, name="shifted")
+        inv = keep.tile([P, PACK], F32, name="inv")
+        cited = [keep.tile([P, S], F32, name="cited%d" % t, align_bytes=64) for t in range(PACK)]
+        mixed = [keep.tile([P, S], F32, name="mixed%d" % t, align_bytes=64) for t in range(PACK)]
+
+        def ker_at(t, width):
+            start = (PACK - 1 - t) * S
+            return ker[:, start : start + width]
+
+        def squash(t, h):
+            if h is not None:
+                nc.scalar.activation(th[t][:, halves[h]], y[t, h], ACT.Tanh)
+            elif t < 3:
+                nc.scalar.activation(th[t][:], y[t][:], ACT.Tanh)
+            else:
+                nc.scalar.activation(last_th, y[t][:].rearrange("p (r c) -> p r c", c=64), ACT.Tanh)
+
+        def grow(t):
+            if t < 3:
+                nc.scalar.activation(ker_at(t, S), th[t][:], ACT.Exp, scale=1.2, accum_out=sums[:, t : t + 1])
+            else:
+                nc.scalar.activation(
+                    ker_at(t, S).rearrange("p (r c) -> p r c", c=64), last_th, ACT.Exp, scale=1.2, accum_out=sums[:, t : t + 1]
+                )
+
+        def cite(t):
+            col = slice(t, t + 1)
+            nc.vector.tensor_scalar(shifted[:, col], sums[:, col], 1.0 / S, 0.3, MULT, ADD)
+            nc.vector.tensor_copy(cited[t][:], ker_at(t, S + SPARE).indirect(cit_sb[:]))
+            nc.vector.reciprocal(inv[:, col], shifted[:, col])
+            nc.vector.scalar_tensor_tensor(mixed[t][:], cited[t][:], 0.6, ker_at(t, S), MULT, ADD)
+
+        squash(0, 0)
+        squash(1, 0)
+        squash(0, 1)
+        grow(0)
+        squash(1, 1)
+        squash(2, None)
+        grow(1)
+        squash(3, None)
+        grow(2)
+        grow(3)
+        for t in range(PACK):
+            cite(t)
+
+        planes = [keep.tile([P, PACK, HALF], BF16, name="planes%d" % h, align_bytes=64) for h in range(2)]
+        woven = [keep.tile([P, HALF, PACK], BF16, name="woven%d" % h, align_bytes=64) for h in range(2)]
+        hid_codes = [keep.tile([P, HALF], U32, name="hid_codes%d" % h, align_bytes=64) for h in range(2)]
+        hid_scales = [keep.tile([P, HALF], U8, name="hid_scales%d" % h, align_bytes=64) for h in range(2)]
+        result = [keep.tile([P, HALF], F32, name="result%d" % h, align_bytes=64) for h in range(2)]
+
+        for t in range(PACK):
+            for h in range(2):
+                nc.scalar.activation(logs[:, t, halves[h]], mixed[t][:, halves[h]], ACT.Ln, bias=0.3, scale=inv[:, t : t + 1])
+        for h in range(2):
+            for t in range(PACK):
+                nc.vector.scalar_tensor_tensor(
+                    planes[h][:, t, :], logs[:, t, halves[h]], unit_sb[:, t : t + 1], y[t, h], MULT, MULT
+                )
+        views = [
+            (woven[h][:].rearrange("p (c i) t -> p c t i", i=4), planes[h][:].rearrange("p t (c i) -> p c t i", i=4))
+            for h in range(2)
+        ]
+        nc.scalar.copy(*views[0])
+        nc.vector.tensor_copy(*views[1])
+        for h in range(2):
+            nc.vector.quantize_mx(
+                hid_codes[h][:].bitcast(FP8X4), hid_scales[h][:], woven[h][:].rearrange("p c t -> p (c t)")
+            )
+            topics = psum.tile([P, HALF], F32, name="topics%d" % h)
+            nc.tensor.matmul_mx(
+                topics[:],
+                lhsT=w_codes[:].bitcast(FP8X4),
+                lhsT_scale=w_scales[:],
+                rhs=hid_codes[h][:].bitcast(FP8X4),
+                rhs_scale=hid_scales[h][:],
+                start=True,
+                stop=True,
+            )
+            nc.scalar.copy(result[h][:], topics[:])
+            nc.sync.dma_start(out[:, halves[h]], result[h][:])

@@ -38,18 +38,26 @@ def tile_picked_yanchr_log_p_kernel(tc, x_words, x_scales, hT, unit, w1, offs, c
         w_raw = keep.tile([P, PACK, N], F32, name="w_raw", align_bytes=64)
         unit_sb = keep.tile([P, PACK], F32, name="unit_sb")
 
-        nc.gpsimd.memset(x_bytes[:].bitcast(I32), 0)
-        nc.sync.dma_start(offs_sb[:], offs)
+        x_rows = keep.tile([P, T // 4], I32, name="x_rows", align_bytes=64)
+        nc.vector.memset(x_bytes[:].bitcast(I32), 0)
+        h_rows = hT.rearrange("(p j) i -> p j i", j=PACK)
+        nc.sync.dma_start(h_raw[:, 0:1, :], h_rows[:, 0:1, :])
         for q in range(4):
-            nc.scalar.dma_start(x_bytes[32 * q : 32 * q + 4, :].bitcast(I32), x_scales[0, 4 * q : 4 * q + 4, :].bitcast(I32))
-        nc.sync.dma_start(h_raw[:], hT.rearrange("(p j) i -> p j i", j=PACK))
+            nc.sync.dma_start(x_rows[32 * q : 32 * q + 4, :], x_scales[0, 4 * q : 4 * q + 4, :].bitcast(I32))
+        nc.sync.dma_start(offs_sb[:], offs)
+        nc.sync.dma_start(h_raw[:, 1:PACK, :], h_rows[:, 1:PACK, :])
+        for q in range(4):
+            nc.vector.tensor_copy(x_bytes[32 * q : 32 * q + 4, :].bitcast(I32), x_rows[32 * q : 32 * q + 4, :])
+        picked_bytes = keep.tile([P, S], U8, name="picked_bytes", align_bytes=64)
+        nc.vector.tensor_copy(picked_bytes[:], x_bytes[:].indirect(offs_sb[:]))
         nc.sync.dma_start(x_table[:], x_words[0].rearrange("p n t -> p (n t)").bitcast(I32))
         nc.sync.dma_start(cit_sb[:], cit)
         nc.sync.dma_start(w_raw[:], w1.rearrange("(p j) m -> p j m", j=PACK))
         nc.sync.dma_start(unit_sb[:], unit.rearrange("(p t) o -> p (t o)", t=PACK))
 
-        ker = keep.tile([P, PACK * S + SPARE], F32, name="ker", align_bytes=64)
-        nc.gpsimd.memset(ker[:, PACK * S :], 0.0)
+        wide = [keep.tile([P, 4 * S], F32, name="wide%d" % t, align_bytes=64) for t in range(3)]
+        narrow = keep.tile([P, S + SPARE], F32, name="narrow", align_bytes=64)
+        ker = [wide[0][:, 0:S], wide[1][:, 0:S], wide[2][:, 0:S], narrow[:, 0:S]]
 
         h_view = h_raw[:].rearrange("p j (m t) -> p m t j", t=PACK)
         h_codes, h_scales = [], []
@@ -62,8 +70,6 @@ def tile_picked_yanchr_log_p_kernel(tc, x_words, x_scales, hT, unit, w1, offs, c
         nc.scalar.activation(h_bf[1][:].rearrange("p t m j -> p m t j"), h_view[:, :, 2:4, :], ACT.Copy)
         nc.vector.quantize_mx(h_codes[0][:].bitcast(FP8X4), h_scales[0][:], h_bf[0][:].rearrange("p t m j -> p (t m j)"))
 
-        picked_bytes = keep.tile([P, S], U8, name="picked_bytes", align_bytes=64)
-        nc.vector.tensor_copy(picked_bytes[:], x_bytes[:].indirect(offs_sb[:]))
         picked_words = []
         for h in range(2):
             words = keep.tile([P, HALF], U32, name="picked_words%d" % h, align_bytes=64)
@@ -105,7 +111,7 @@ def tile_picked_yanchr_log_p_kernel(tc, x_words, x_scales, hT, unit, w1, offs, c
         nc.vector.quantize_mx(w_codes[:].bitcast(FP8X4), w_scales[:], w_bf[:].rearrange("p m j -> p (m j)"))
 
         logs = keep.tile([P, PACK, S], F32, name="logs", align_bytes=64)
-        th = [keep.tile([P, S], F32, name="th%d" % t, align_bytes=64) for t in range(3)]
+        th = [wide[t][:, S : 2 * S] for t in range(3)]
         last_th = logs[:].rearrange("p t (h c) -> p (t h) c", h=2)[:, :, 0:64]
         sums = keep.tile([P, PACK], F32, name="sums")
         shifted = keep.tile([P, PACK], F32, name="shifted")
@@ -113,32 +119,34 @@ def tile_picked_yanchr_log_p_kernel(tc, x_words, x_scales, hT, unit, w1, offs, c
         cited = [keep.tile([P, S], F32, name="cited%d" % t, align_bytes=64) for t in range(PACK)]
         mixed = [keep.tile([P, S], F32, name="mixed%d" % t, align_bytes=64) for t in range(PACK)]
 
-        def ker_at(t, width):
-            start = (PACK - 1 - t) * S
-            return ker[:, start : start + width]
-
         def squash(t, h):
             if h is not None:
                 nc.scalar.activation(th[t][:, halves[h]], y[t, h], ACT.Tanh)
             elif t < 3:
-                nc.scalar.activation(th[t][:], y[t][:], ACT.Tanh)
+                nc.scalar.activation(th[t], y[t][:], ACT.Tanh)
             else:
                 nc.scalar.activation(last_th, y[t][:].rearrange("p (r c) -> p r c", c=64), ACT.Tanh)
 
         def grow(t):
             if t < 3:
-                nc.scalar.activation(ker_at(t, S), th[t][:], ACT.Exp, scale=1.2, accum_out=sums[:, t : t + 1])
+                nc.scalar.activation(ker[t], th[t], ACT.Exp, scale=1.2, accum_out=sums[:, t : t + 1])
             else:
                 nc.scalar.activation(
-                    ker_at(t, S).rearrange("p (r c) -> p r c", c=64), last_th, ACT.Exp, scale=1.2, accum_out=sums[:, t : t + 1]
+                    ker[t].rearrange("p (r c) -> p r c", c=64), last_th, ACT.Exp, scale=1.2, accum_out=sums[:, t : t + 1]
                 )
 
         def cite(t):
             col = slice(t, t + 1)
             nc.vector.tensor_scalar(shifted[:, col], sums[:, col], 1.0 / S, 0.3, MULT, ADD)
-            nc.vector.tensor_copy(cited[t][:], ker_at(t, S + SPARE).indirect(cit_sb[:]))
+            if t < 3:
+                nc.vector.tensor_scalar(cited[t][:], wide[t][:].indirect(cit_sb[:]), 0.6, 0.0, MULT, ADD)
+            else:
+                nc.vector.tensor_copy(cited[t][:], narrow[:].indirect(cit_sb[:]))
             nc.vector.reciprocal(inv[:, col], shifted[:, col])
-            nc.vector.scalar_tensor_tensor(mixed[t][:], cited[t][:], 0.6, ker_at(t, S), MULT, ADD)
+            if t < 3:
+                nc.gpsimd.tensor_tensor(mixed[t][:], cited[t][:], ker[t], ADD)
+            else:
+                nc.vector.scalar_tensor_tensor(mixed[t][:], cited[t][:], 0.6, ker[t], MULT, ADD)
 
         squash(0, 0)
         squash(1, 0)
@@ -159,8 +167,8 @@ def tile_picked_yanchr_log_p_kernel(tc, x_words, x_scales, hT, unit, w1, offs, c
         hid_scales = [keep.tile([P, HALF], U8, name="hid_scales%d" % h, align_bytes=64) for h in range(2)]
         result = [keep.tile([P, HALF], F32, name="result%d" % h, align_bytes=64) for h in range(2)]
 
-        for t in range(PACK):
-            for h in range(2):
+        for h in range(2):
+            for t in range(PACK):
                 nc.scalar.activation(logs[:, t, halves[h]], mixed[t][:, halves[h]], ACT.Ln, bias=0.3, scale=inv[:, t : t + 1])
         for h in range(2):
             for t in range(PACK):

@@ -19,7 +19,6 @@ ADD = mybir.AluOpType.add
 P = 128
 PACK = 4
 HALF = S // 2
-SPARE = 192
 
 
 def tile_picked_yanchr_log_p_kernel(tc, x_words, x_scales, hT, unit, w1, offs, cit, out):
@@ -40,24 +39,23 @@ def tile_picked_yanchr_log_p_kernel(tc, x_words, x_scales, hT, unit, w1, offs, c
 
         x_rows = keep.tile([P, T // 4], I32, name="x_rows", align_bytes=64)
         nc.vector.memset(x_bytes[:].bitcast(I32), 0)
-        h_rows = hT.rearrange("(p j) i -> p j i", j=PACK)
-        nc.sync.dma_start(h_raw[:, 0:1, :], h_rows[:, 0:1, :])
+        x_flat = x_words[0].rearrange("p n t -> p (n t)").bitcast(I32)
+        nc.sync.dma_start(x_table[:, 0 : T // 4], x_flat[:, 0 : T // 4])
         for q in range(4):
             nc.sync.dma_start(x_rows[32 * q : 32 * q + 4, :], x_scales[0, 4 * q : 4 * q + 4, :].bitcast(I32))
         nc.sync.dma_start(offs_sb[:], offs)
-        nc.sync.dma_start(h_raw[:, 1:PACK, :], h_rows[:, 1:PACK, :])
+        nc.sync.dma_start(h_raw[:], hT.rearrange("(p j) i -> p j i", j=PACK))
         for q in range(4):
             nc.vector.tensor_copy(x_bytes[32 * q : 32 * q + 4, :].bitcast(I32), x_rows[32 * q : 32 * q + 4, :])
         picked_bytes = keep.tile([P, S], U8, name="picked_bytes", align_bytes=64)
         nc.vector.tensor_copy(picked_bytes[:], x_bytes[:].indirect(offs_sb[:]))
-        nc.sync.dma_start(x_table[:], x_words[0].rearrange("p n t -> p (n t)").bitcast(I32))
+        nc.sync.dma_start(x_table[:, T // 4 :], x_flat[:, T // 4 :])
         nc.sync.dma_start(cit_sb[:], cit)
         nc.sync.dma_start(w_raw[:], w1.rearrange("(p j) m -> p j m", j=PACK))
         nc.sync.dma_start(unit_sb[:], unit.rearrange("(p t) o -> p (t o)", t=PACK))
 
-        wide = [keep.tile([P, 4 * S], F32, name="wide%d" % t, align_bytes=64) for t in range(3)]
-        narrow = keep.tile([P, S + SPARE], F32, name="narrow", align_bytes=64)
-        ker = [wide[0][:, 0:S], wide[1][:, 0:S], wide[2][:, 0:S], narrow[:, 0:S]]
+        wide = [keep.tile([P, 4 * S], F32, name="wide%d" % t, align_bytes=64) for t in range(PACK)]
+        ker = [wide[t][:, 0:S] for t in range(PACK)]
 
         h_view = h_raw[:].rearrange("p j (m t) -> p m t j", t=PACK)
         h_codes, h_scales = [], []
@@ -138,15 +136,13 @@ def tile_picked_yanchr_log_p_kernel(tc, x_words, x_scales, hT, unit, w1, offs, c
         def cite(t):
             col = slice(t, t + 1)
             nc.vector.tensor_scalar(shifted[:, col], sums[:, col], 1.0 / S, 0.3, MULT, ADD)
-            if t < 3:
-                nc.vector.tensor_scalar(cited[t][:], wide[t][:].indirect(cit_sb[:]), 0.6, 0.0, MULT, ADD)
-            else:
-                nc.vector.tensor_copy(cited[t][:], narrow[:].indirect(cit_sb[:]))
+            nc.vector.tensor_scalar(cited[t][:], wide[t][:].indirect(cit_sb[:]), 0.6, 0.0, MULT, ADD)
             nc.vector.reciprocal(inv[:, col], shifted[:, col])
-            if t < 3:
+            if t < PACK - 1:
                 nc.gpsimd.tensor_tensor(mixed[t][:], cited[t][:], ker[t], ADD)
             else:
-                nc.vector.scalar_tensor_tensor(mixed[t][:], cited[t][:], 0.6, ker[t], MULT, ADD)
+                nc.vector.tensor_tensor(mixed[t][:, halves[0]], cited[t][:, halves[0]], ker[t][:, halves[0]], ADD)
+                nc.gpsimd.tensor_tensor(mixed[t][:, halves[1]], cited[t][:, halves[1]], ker[t][:, halves[1]], ADD)
 
         squash(0, 0)
         squash(1, 0)
@@ -167,14 +163,13 @@ def tile_picked_yanchr_log_p_kernel(tc, x_words, x_scales, hT, unit, w1, offs, c
         hid_scales = [keep.tile([P, HALF], U8, name="hid_scales%d" % h, align_bytes=64) for h in range(2)]
         result = [keep.tile([P, HALF], F32, name="result%d" % h, align_bytes=64) for h in range(2)]
 
-        for h in range(2):
-            for t in range(PACK):
-                nc.scalar.activation(logs[:, t, halves[h]], mixed[t][:, halves[h]], ACT.Ln, bias=0.3, scale=inv[:, t : t + 1])
-        for h in range(2):
-            for t in range(PACK):
-                nc.vector.scalar_tensor_tensor(
-                    planes[h][:, t, :], logs[:, t, halves[h]], unit_sb[:, t : t + 1], y[t, h], MULT, MULT
-                )
+        order = [(t, h) for h in range(2) for t in range(PACK)]
+        for t, h in order:
+            nc.scalar.activation(logs[:, t, halves[h]], mixed[t][:, halves[h]], ACT.Ln, bias=0.3, scale=inv[:, t : t + 1])
+        for t, h in order:
+            nc.vector.scalar_tensor_tensor(
+                planes[h][:, t, :], logs[:, t, halves[h]], unit_sb[:, t : t + 1], y[t, h], MULT, MULT
+            )
         views = [
             (woven[h][:].rearrange("p (c i) t -> p c t i", i=4), planes[h][:].rearrange("p t (c i) -> p c t i", i=4))
             for h in range(2)

from contextlib import ExitStack

import concourse.mybir as mybir

K, T, S, N, H = 512, 2048, 512, 128, 512
FLOPS = 2 * K * H * S + 2 * H * N * S

F32 = mybir.dt.float32
BF16 = mybir.dt.bfloat16
I32 = mybir.dt.int32
U32 = mybir.dt.uint32
U16 = mybir.dt.uint16
U8 = mybir.dt.uint8
FP8X4 = mybir.dt.float8_e4m3fn_x4
ACT = mybir.ActivationFunctionType
MULT = mybir.AluOpType.mult
ADD = mybir.AluOpType.add

P = 128
PACK = 4
HALF = S // 2


def tile_picked_yanchr_log_p_kernel(tc, x_words, x_scales, hT, unit, w1, offs, cit, out):
    nc = tc.nc
    with ExitStack() as ctx:
        keep = ctx.enter_context(tc.tile_pool(name="keep", bufs=1))
        psum = ctx.enter_context(tc.psum_pool(name="psum", bufs=1))

        halves = [slice(0, HALF), slice(HALF, S)]

        offs_sb = keep.tile([P, S // 16], U16, name="offs_sb")
        cit_sb = keep.tile([P, S // 16], U16, name="cit_sb")
        x_bytes = keep.tile([P, T], U8, name="x_bytes", align_bytes=64)
        x_table = keep.tile([P, T], I32, name="x_table", align_bytes=64)
        h_raw = keep.tile([P, PACK, H], F32, name="h_raw", align_bytes=64)
        w_raw = keep.tile([P, PACK, N], F32, name="w_raw", align_bytes=64)
        unit_sb = keep.tile([P, PACK], F32, name="unit_sb")

        x_rows = keep.tile([P, T // 4], I32, name="x_rows", align_bytes=64)
        nc.vector.memset(x_bytes[:].bitcast(I32), 0)
        x_flat = x_words[0].rearrange("p n t -> p (n t)").bitcast(I32)
        nc.sync.dma_start(x_table[:, 0 : T // 4], x_flat[:, 0 : T // 4])
        for q in range(4):
            nc.sync.dma_start(x_rows[32 * q : 32 * q + 4, :], x_scales[0, 4 * q : 4 * q + 4, :].bitcast(I32))
        nc.sync.dma_start(offs_sb[:], offs)
        nc.sync.dma_start(h_raw[:], hT.rearrange("(p j) i -> p j i", j=PACK))
        for q in range(4):
            nc.vector.tensor_copy(x_bytes[32 * q : 32 * q + 4, :].bitcast(I32), x_rows[32 * q : 32 * q + 4, :])
        picked_bytes = keep.tile([P, S], U8, name="picked_bytes", align_bytes=64)
        nc.vector.tensor_copy(picked_bytes[:], x_bytes[:].indirect(offs_sb[:]))
        nc.sync.dma_start(x_table[:, T // 4 :], x_flat[:, T // 4 :])
        nc.sync.dma_start(cit_sb[:], cit)
        nc.sync.dma_start(w_raw[:], w1.rearrange("(p j) m -> p j m", j=PACK))
        nc.sync.dma_start(unit_sb[:], unit.rearrange("(p t) o -> p (t o)", t=PACK))

        wide = [keep.tile([P, 4 * S], F32, name="wide%d" % t, align_bytes=64) for t in range(PACK)]
        ker = [wide[t][:, 0:S] for t in range(PACK)]

        h_view = h_raw[:].rearrange("p j (m t) -> p m t j", t=PACK)
        h_codes, h_scales = [], []
        h_bf = []
        for pair in range(2):
            h_bf.append(keep.tile([P, 2, P, PACK], BF16, name="h_bf%d" % pair, align_bytes=64))
            h_codes.append(keep.tile([P, 2 * P], U32, name="h_codes%d" % pair, align_bytes=64))
            h_scales.append(keep.tile([P, 2 * P], U8, name="h_scales%d" % pair, align_bytes=64))
        nc.vector.tensor_copy(h_bf[0][:].rearrange("p t m j -> p m t j"), h_view[:, :, 0:2, :])
        nc.scalar.activation(h_bf[1][:].rearrange("p t m j -> p m t j"), h_view[:, :, 2:4, :], ACT.Copy)
        nc.vector.quantize_mx(h_codes[0][:].bitcast(FP8X4), h_scales[0][:], h_bf[0][:].rearrange("p t m j -> p (t m j)"))

        picked_words = []
        for h in range(2):
            words = keep.tile([P, HALF], U32, name="picked_words%d" % h, align_bytes=64)
            nc.vector.tensor_copy(words[:], x_table[:].bitcast(U32).indirect(offs_sb[:, 16 * h : 16 * h + 16]))
            picked_words.append(words)
        nc.vector.quantize_mx(h_codes[1][:].bitcast(FP8X4), h_scales[1][:], h_bf[1][:].rearrange("p t m j -> p (t m j)"))

        y = {}
        for t in range(2):
            for h in range(2):
                y[t, h] = psum.tile([P, HALF], F32, name="y%d%d" % (t, h))[:]
        for t in range(2, 4):
            bank = psum.tile([P, S], F32, name="y%d" % t)
            y[t] = bank
            for h in range(2):
                y[t, h] = bank[:, halves[h]]

        def product(t, h):
            cols = slice((t % 2) * P, (t % 2 + 1) * P)
            nc.tensor.matmul_mx(
                y[t, h],
                lhsT=h_codes[t // 2][:, cols].bitcast(FP8X4),
                lhsT_scale=h_scales[t // 2][:, cols],
                rhs=picked_words[h][:].bitcast(FP8X4),
                rhs_scale=picked_bytes[:, halves[h]],
                start=True,
                stop=True,
            )

        for t, h in ((0, 0), (1, 0), (0, 1), (1, 1), (2, 0), (2, 1), (3, 0), (3, 1)):
            product(t, h)

        w_bf = keep.tile([P, N, PACK], BF16, name="w_bf", align_bytes=64)
        w_codes = keep.tile([P, N], U32, name="w_codes", align_bytes=64)
        w_scales = keep.tile([P, N], U8, name="w_scales", align_bytes=64)
        nc.vector.tensor_copy(
            w_bf[:].rearrange("p (c i) j -> p c j i", i=4), w_raw[:].rearrange("p j (c i) -> p c j i", i=4)
        )
        nc.vector.quantize_mx(w_codes[:].bitcast(FP8X4), w_scales[:], w_bf[:].rearrange("p m j -> p (m j)"))

        logs = keep.tile([P, PACK, S], F32, name="logs", align_bytes=64)
        th = [wide[t][:, S : 2 * S] for t in range(3)]
        last_th = logs[:].rearrange("p t (h c) -> p (t h) c", h=2)[:, :, 0:64]
        sums = keep.tile([P, PACK], F32, name="sums")
        shifted = keep.tile([P, PACK], F32, name="shifted")
        inv = keep.tile([P, PACK], F32, name="inv")
        cited = [keep.tile([P, S], F32, name="cited%d" % t, align_bytes=64) for t in range(PACK)]
        mixed = [keep.tile([P, S], F32, name="mixed%d" % t, align_bytes=64) for t in range(PACK)]

        def squash(t, h):
            if h is not None:
                nc.scalar.activation(th[t][:, halves[h]], y[t, h], ACT.Tanh)
            elif t < 3:
                nc.scalar.activation(th[t], y[t][:], ACT.Tanh)
            else:
                nc.scalar.activation(last_th, y[t][:].rearrange("p (r c) -> p r c", c=64), ACT.Tanh)

        def grow(t):
            if t < 3:
                nc.scalar.activation(ker[t], th[t], ACT.Exp, scale=1.2, accum_out=sums[:, t : t + 1])
            else:
                nc.scalar.activation(
                    ker[t].rearrange("p (r c) -> p r c", c=64), last_th, ACT.Exp, scale=1.2, accum_out=sums[:, t : t + 1]
                )

        def cite(t):
            col = slice(t, t + 1)
            nc.vector.tensor_scalar(shifted[:, col], sums[:, col], 1.0 / S, 0.3, MULT, ADD)
            nc.vector.tensor_scalar(cited[t][:], wide[t][:].indirect(cit_sb[:]), 0.6, 0.0, MULT, ADD)
            nc.vector.reciprocal(inv[:, col], shifted[:, col])
            if t < PACK - 1:
                nc.gpsimd.tensor_tensor(mixed[t][:], cited[t][:], ker[t], ADD)
            else:
                nc.vector.tensor_tensor(mixed[t][:, halves[0]], cited[t][:, halves[0]], ker[t][:, halves[0]], ADD)
                nc.gpsimd.tensor_tensor(mixed[t][:, halves[1]], cited[t][:, halves[1]], ker[t][:, halves[1]], ADD)

        squash(0, 0)
        squash(1, 0)
        squash(0, 1)
        grow(0)
        squash(1, 1)
        squash(2, None)
        grow(1)
        squash(3, None)
        grow(2)
        grow(3)
        for t in range(PACK):
            cite(t)

        planes = [keep.tile([P, PACK, HALF], BF16, name="planes%d" % h, align_bytes=64) for h in range(2)]
        woven = [keep.tile([P, HALF, PACK], BF16, name="woven%d" % h, align_bytes=64) for h in range(2)]
        hid_codes = [keep.tile([P, HALF], U32, name="hid_codes%d" % h, align_bytes=64) for h in range(2)]
        hid_scales = [keep.tile([P, HALF], U8, name="hid_scales%d" % h, align_bytes=64) for h in range(2)]
        result = [keep.tile([P, HALF], F32, name="result%d" % h, align_bytes=64) for h in range(2)]

        order = [(t, h) for h in range(2) for t in range(PACK)]
        for t, h in order:
            nc.scalar.activation(logs[:, t, halves[h]], mixed[t][:, halves[h]], ACT.Ln, bias=0.3, scale=inv[:, t : t + 1])
        for t, h in order:
            nc.vector.scalar_tensor_tensor(
                planes[h][:, t, :], logs[:, t, halves[h]], unit_sb[:, t : t + 1], y[t, h], MULT, MULT
            )
        views = [
            (woven[h][:].rearrange("p (c i) t -> p c t i", i=4), planes[h][:].rearrange("p t (c i) -> p c t i", i=4))
            for h in range(2)
        ]
        nc.scalar.copy(*views[0])
        nc.vector.tensor_copy(*views[1])
        for h in range(2):
            nc.vector.quantize_mx(
                hid_codes[h][:].bitcast(FP8X4), hid_scales[h][:], woven[h][:].rearrange("p c t -> p (c t)")
            )
            topics = psum.tile([P, HALF], F32, name="topics%d" % h)
            nc.tensor.matmul_mx(
                topics[:],
                lhsT=w_codes[:].bitcast(FP8X4),
                lhsT_scale=w_scales[:],
                rhs=hid_codes[h][:].bitcast(FP8X4),
                rhs_scale=hid_scales[h][:],
                start=True,
                stop=True,
            )
            nc.scalar.copy(result[h][:], topics[:])
            nc.sync.dma_start(out[:, halves[h]], result[h][:])
